import numpy as np
import ml_dtypes


def mxq(x, axis, fmt="e4m3"):
    dtype, down = {"e4m3": (ml_dtypes.float8_e4m3fn, 7), "e5m2": (ml_dtypes.float8_e5m2, 14)}[fmt]
    v = np.moveaxis(np.asarray(x, np.float32).astype(ml_dtypes.bfloat16).astype(np.float64), axis, -1)
    blocks = v.reshape(v.shape[:-1] + (-1, 32))
    amax = np.abs(blocks).max(-1, keepdims=True)
    byte = np.maximum(np.where(amax > 0, np.frexp(amax)[1] - 1 + 127, 0) - down, 1)
    scale = np.exp2(byte - 127.0)
    codes = (blocks / scale).astype(np.float32).astype(dtype).astype(np.float64)
    return np.moveaxis((codes * scale).reshape(v.shape), -1, axis)


WIDE = False


def mx_kscale(k):
    if not WIDE:
        return np.ones(k)
    levels = np.array([30, -30])
    if k % 512:
        return np.exp2(np.random.permutation(np.resize(levels, k // 32))).repeat(32)
    a = np.empty((k // 512, 16))
    for p in range(k // 512):
        a[p, :8] = np.random.permutation(np.resize(levels, 8))
        for g in range(8):
            far = levels[np.abs(levels - a[p, g]) >= 10]
            a[p, g + 8] = far[np.random.randint(len(far))]
    return np.exp2(a.ravel()).repeat(32)


def f64(x):
    return np.asarray(x).astype(np.float64)


def striped(idx):
    return np.tile(np.asarray(idx).reshape(-1, 16).T, (8, 1)).astype(np.uint16)


def unstriped(offs):
    return offs[:16].T.reshape(-1).astype(np.int64)


E2M1 = np.array([0.0, 0.5, 1.0, 1.5, 2.0, 3.0, 4.0, 6.0, -0.0, -0.5, -1.0, -1.5, -2.0, -3.0, -4.0, -6.0])


def pack_weight(w, fmt):
    k, n = w.shape
    w = f64(np.asarray(w, np.float32).astype(ml_dtypes.bfloat16)).reshape(k // 32, 32, n)
    amax = np.abs(w).max(1)
    if fmt in ("e4m3", "e5m2"):
        byte = np.frexp(amax)[1] - 1 + 127 - (7 if fmt == "e4m3" else 14)
    else:
        mant, ex = np.frexp(amax / 6.0)
        byte = np.where(mant > 0.5, ex, ex - 1) + 127
    byte = np.clip(np.where(amax > 0, byte, 1), 1, 254)
    scaled = (w * np.exp2(127.0 - byte)[:, None, :]).reshape(k, n).astype(np.float32)
    by_word = np.ascontiguousarray(scaled.reshape(k // 512, 128, 4, n).transpose(0, 1, 3, 2))
    if fmt in ("e4m3", "e5m2"):
        words = by_word.astype(ml_dtypes.float8_e4m3fn if fmt == "e4m3" else ml_dtypes.float8_e5m2).view(np.uint8)
    else:
        c = by_word.astype(ml_dtypes.float4_e2m1fn).view(np.uint8) & 0xF
        words = (c[..., 0::2] | (c[..., 1::2] << 4)).reshape(k // 512, 128, 2 * n)
    return np.ascontiguousarray(words), np.ascontiguousarray(byte.astype(np.uint8).reshape(k // 512, 16, n))


def unpack_weight(words, scales, fmt):
    g, _, n = scales.shape
    words = np.ascontiguousarray(words).reshape(g, 128, n, -1)
    if fmt in ("e4m3", "e5m2"):
        vals = words.view(ml_dtypes.float8_e4m3fn if fmt == "e4m3" else ml_dtypes.float8_e5m2).astype(np.float64)
    else:
        nib = np.empty((g, 128, n, 4), np.uint8)
        nib[..., 0::2] = words & 0xF
        nib[..., 1::2] = words >> 4
        vals = E2M1[nib]
    vals = vals * np.repeat(np.exp2(scales.astype(np.float64) - 127.0), 8, axis=1)[..., None]
    return vals.transpose(0, 1, 3, 2).reshape(g * 512, n)


def sigmoid(v):
    return 1.0 / (1.0 + np.exp(-v))


def sgn(shape):
    return np.random.uniform(0.5, 2.0, shape) * np.where(np.random.standard_normal(shape) < 0, -1.0, 1.0)


K, T, J, R, F, Z, I, O, N, E = 512, 1024, 256, 512, 512, 1024, 256, 128, 256, 1024


def setup_inputs():
    n = np.random.standard_normal
    idx = np.random.permutation(T)[:J]
    idx2 = np.random.permutation(Z)[:J]
    idx3 = np.random.permutation(J)[:I]
    idx4 = np.random.permutation(J)[:I]
    idx5 = np.random.permutation(T)[:O]
    idx6 = np.random.permutation(E)[:O]
    fk = mx_kscale(K)
    ff = mx_kscale(F)
    fr = mx_kscale(R)
    xtp = pack_weight(n((K, T)) / fk[:, None], "e2m1")
    xop = pack_weight(n((F, Z)) / ff[:, None], "e5m2")
    wp = pack_weight(n((K, R)) * 1 / np.sqrt(K) * fk[:, None], "e5m2")
    w0p = pack_weight(n((F, R)) * 1 / np.sqrt(F) * ff[:, None], "e4m3")
    wbp = pack_weight(n((R, N)) * 1 / np.sqrt(R) / fr[:, None], "e4m3")
    wsp = pack_weight(n((K, N)) * 1 / np.sqrt(K) * fk[:, None], "e4m3")
    return {
        "xt_words": xtp[0],
        "xt_scales": xtp[1],
        "xo_words": xop[0],
        "xo_scales": xop[1],
        "w_words": wp[0],
        "w_scales": wp[1],
        "w0_words": w0p[0],
        "w0_scales": w0p[1],
        "sa": (sgn((R, 1)) * fr[:, None]).astype(np.float32),
        "sg": (sgn((R, 1))).astype(np.float32),
        "bg": (np.random.uniform(-2.0, 2.0, (R, 1))).astype(np.float32),
        "wb_words": wbp[0],
        "wb_scales": wbp[1],
        "ws_words": wsp[0],
        "ws_scales": wsp[1],
        "offs": striped(idx),
        "offs2": striped(idx2),
        "offs3": striped(idx3),
        "offs4": striped(idx4),
        "offs5": striped(idx5),
        "offs6": striped(idx6),
    }


def reference(xt_words, xt_scales, xo_words, xo_scales, w_words, w_scales, w0_words, w0_scales, sa, sg, bg, wb_words, wb_scales, ws_words, ws_scales, offs, offs2, offs3, offs4, offs5, offs6):
    idx = unstriped(offs)
    idx2 = unstriped(offs2)
    idx3 = unstriped(offs3)
    idx4 = unstriped(offs4)
    idx5 = unstriped(offs5)
    idx6 = unstriped(offs6)
    xtu = unpack_weight(xt_words, xt_scales, "e2m1")
    xou = unpack_weight(xo_words, xo_scales, "e5m2")
    wu = unpack_weight(w_words, w_scales, "e5m2")
    w0u = unpack_weight(w0_words, w0_scales, "e4m3")
    wbu = unpack_weight(wb_words, wb_scales, "e4m3")
    wsu = unpack_weight(ws_words, ws_scales, "e4m3")
    xtidxg = xtu[:, idx]
    xoidx2g = xou[:, idx2]
    a = wu.T @ xtidxg + w0u.T @ xoidx2g
    h1 = a[:, idx3] * f64(sa) * sigmoid(a[:, idx4] * f64(sg) + f64(bg))
    hid = h1.reshape(R, O, I // O).max(axis=2)
    hidq = mxq(hid, 0, "e5m2")
    xtidx5g = xtu[:, idx5]
    p = wbu.T @ hidq + wsu.T @ xtidx5g
    y = np.zeros((N, E))
    y[:, idx6] = p
    return y

@@ -1,0 +1,199 @@
+from contextlib import ExitStack
+
+import concourse.mybir as mybir
+
+K, T, J, R, F, Z, I, O, N, E = 512, 1024, 256, 512, 512, 1024, 256, 128, 256, 1024
+FLOPS = 2 * (K * R * J + F * R * J + R * N * O + K * N * O)
+
+F32 = mybir.dt.float32
+BF16 = mybir.dt.bfloat16
+I32 = mybir.dt.int32
+U32 = mybir.dt.uint32
+U16 = mybir.dt.uint16
+U8 = mybir.dt.uint8
+E4M3 = mybir.dt.float8_e4m3fn_x4
+E5M2 = mybir.dt.float8_e5m2_x4
+E2M1 = mybir.dt.float4_e2m1fn_x4
+ACT = mybir.ActivationFunctionType
+ALU = mybir.AluOpType
+
+P = 128
+PACK = 4
+WHOLE = 2
+PICK_PARTS = ((0, 128), (128, 192), (192, 256))
+
+
+def tile_list_gatedpool_bank_further_scattered_kernel(
+    tc, xt_words, xt_scales, xo_words, xo_scales, w_words, w_scales, w0_words, w0_scales,
+    sa, sg, bg, wb_words, wb_scales, ws_words, ws_scales,
+    offs, offs2, offs3, offs4, offs5, offs6, out,
+):
+    nc = tc.nc
+    with ExitStack() as ctx:
+        pool = ctx.enter_context(tc.tile_pool(name="held", bufs=1))
+        psum = ctx.enter_context(tc.psum_pool(name="psum", bufs=1))
+
+        def sbuf(name, shape, dtype):
+            return pool.tile(shape, dtype, name=name, align_bytes=64)
+
+        def load_list(name, src):
+            tile = pool.tile(list(src.shape), U16, name=name)
+            nc.sync.dma_start(tile[:], src)
+            return tile
+
+        def load_words(queue, name, src, cols, dtype):
+            tile = sbuf(name, [P, cols], dtype)
+            queue.dma_start(tile[:].bitcast(I32), src.bitcast(I32))
+            return tile
+
+        def flat_words(words):
+            return words[0].rearrange("p n t -> p (n t)")
+
+        def zeroed_plane(name, cols):
+            tile = sbuf(name, [P, cols], U8)
+            nc.vector.memset(tile[:].bitcast(I32), 0)
+            return tile
+
+        def load_plane(queue, tile, scales):
+            for q in range(4):
+                queue.dma_start(tile[32 * q : 32 * q + 4, :].bitcast(I32), scales[0, 4 * q : 4 * q + 4, :].bitcast(I32))
+
+        def load_rows(name, src):
+            tile = pool.tile([P, PACK], F32, name=name)
+            nc.gpsimd.dma_start(tile[:], src.rearrange("(p t) one -> p (t one)", t=PACK))
+            return tile
+
+        xt_plane = zeroed_plane("xt_plane", T)
+        xo_plane = zeroed_plane("xo_plane", Z)
+        w_plane = zeroed_plane("w_plane", R)
+        w0_plane = zeroed_plane("w0_plane", R)
+        ws_plane = zeroed_plane("ws_plane", N)
+        wb_plane = zeroed_plane("wb_plane", N)
+
+        xt_sb = load_words(nc.scalar, "xt_sb", xt_words[0], T, U16)
+        xo_sb = load_words(nc.scalar, "xo_sb", flat_words(xo_words), Z, U32)
+        w_sb = load_words(nc.scalar, "w_sb", flat_words(w_words), R, U32)
+        w0_sb = load_words(nc.scalar, "w0_sb", flat_words(w0_words), R, U32)
+
+        list1 = load_list("list1", offs)
+        load_plane(nc.sync, xt_plane, xt_scales)
+        list2 = load_list("list2", offs2)
+        load_plane(nc.sync, xo_plane, xo_scales)
+        load_plane(nc.sync, w_plane, w_scales)
+        load_plane(nc.sync, w0_plane, w0_scales)
+        sg_sb = load_rows("sg_sb", sg)
+        bg_sb = load_rows("bg_sb", bg)
+        sa_sb = load_rows("sa_sb", sa)
+        list4 = load_list("list4", offs4)
+        list3 = load_list("list3", offs3)
+        list5 = load_list("list5", offs5)
+        ws_sb = load_words(nc.sync, "ws_sb", flat_words(ws_words), N, U32)
+        wb_sb = load_words(nc.sync, "wb_sb", flat_words(wb_words), N, U32)
+        load_plane(nc.sync, ws_plane, ws_scales)
+        load_plane(nc.sync, wb_plane, wb_scales)
+        list6 = load_list("list6", offs6)
+
+        pages = [pool.tile([P, E], F32, name="page%d" % h) for h in range(N // P)]
+        for page in pages:
+            nc.vector.memset(page[:], 0.0)
+
+        def gather(name, table, offsets, cols, dtype):
+            tile = sbuf(name, [P, cols], dtype)
+            nc.vector.tensor_copy(tile[:], table[:].indirect(offsets[:]))
+            return tile
+
+        def deal(copy, name, src, dtype, run, t0, t1):
+            tile = sbuf(name, [P, (t1 - t0) * P], dtype)
+            copy(
+                tile[:].rearrange("p (t c i) -> p c t i", t=t1 - t0, i=run),
+                src[:].rearrange("p (c i t) -> p c t i", t=PACK, i=run)[:, :, t0:t1, :],
+            )
+            return [tile[:, P * t : P * (t + 1)] for t in range(t1 - t0)]
+
+        xt1_plane = gather("xt1_plane", xt_plane, list1, J, U8)
+        xt1_words = gather("xt1_words", xt_sb, list1, J, U16)
+        xo2_plane = gather("xo2_plane", xo_plane, list2, J, U8)
+        xo2_words = gather("xo2_words", xo_sb, list2, J, U32)
+        wd_words = deal(nc.scalar.copy, "wd_words", w_sb, U32, 4, 0, PACK)
+        wd_plane, w0d_plane, w0d_words = [], [], []
+        for t0, t1 in ((0, 1), (1, PACK)):
+            wd_plane.extend(deal(nc.vector.tensor_copy, "wd_plane%d" % t0, w_plane, U8, 16, t0, t1))
+            w0d_plane.extend(deal(nc.vector.tensor_copy, "w0d_plane%d" % t0, w0_plane, U8, 16, t0, t1))
+            w0d_words.extend(deal(nc.scalar.copy, "w0d_words%d" % t0, w0_sb, U32, 4, t0, t1))
+
+        a_rows = []
+        for t in range(PACK):
+            bank = psum.tile([P, J], F32, name="a_bank%d" % t)
+            nc.tensor.matmul_mx(
+                bank[:], lhsT=wd_words[t].bitcast(E5M2), lhsT_scale=wd_plane[t],
+                rhs=xt1_words[:].bitcast(E2M1), rhs_scale=xt1_plane[:], start=True, stop=False,
+            )
+            nc.tensor.matmul_mx(
+                bank[:], lhsT=w0d_words[t].bitcast(E4M3), lhsT_scale=w0d_plane[t],
+                rhs=xo2_words[:].bitcast(E5M2), rhs_scale=xo2_plane[:], start=False, stop=True,
+            )
+            rows = pool.tile([P, 2 * J if t < WHOLE else J], F32, name="a_rows%d" % t)
+            nc.vector.tensor_copy(rows[:, 0:J], bank[:])
+            a_rows.append(rows)
+
+        xt5_plane = gather("xt5_plane", xt_plane, list5, O, U8)
+        xt5_words = gather("xt5_words", xt_sb, list5, O, U16)
+        p_banks = [psum.tile([P, O], F32, name="p_bank%d" % h) for h in range(N // P)]
+        for h in range(N // P):
+            cols = slice(P * h, P * (h + 1))
+            nc.tensor.matmul_mx(
+                p_banks[h][:], lhsT=ws_sb[:, cols].bitcast(E4M3), lhsT_scale=ws_plane[:, cols],
+                rhs=xt5_words[:].bitcast(E2M1), rhs_scale=xt5_plane[:], start=True, stop=False,
+            )
+
+        hid_words = sbuf("hid_words", [P, O], U32)
+        hid_plane = sbuf("hid_plane", [P, O], U8)
+        half = O // 2
+        hid_bf = [sbuf("hid_bf%d" % h, [P, half, PACK], BF16) for h in range(2)]
+
+        def fetch(t, gate, value, entries):
+            nc.scalar.activation(
+                gate, a_rows[t][:].indirect(list4[:, entries]), ACT.Sigmoid,
+                bias=bg_sb[:, t : t + 1], scale=sg_sb[:, t : t + 1],
+            )
+            nc.scalar.activation(
+                value, a_rows[t][:].indirect(list3[:, entries]), ACT.Copy, scale=sa_sb[:, t : t + 1],
+            )
+
+        h1_parts = [pool.tile([P, PACK, hi - lo], F32, name="h1_%d" % lo) for lo, hi in PICK_PARTS]
+        gate_all = pool.tile([P, WHOLE, I], F32, name="gate_all")
+        value_all = pool.tile([P, WHOLE, I], F32, name="value_all")
+        for t in range(WHOLE):
+            fetch(t, gate_all[:, t, :], value_all[:, t, :], slice(0, I // 16))
+        for h1, (lo, hi) in zip(h1_parts, PICK_PARTS):
+            nc.vector.tensor_tensor(h1[:, 0:WHOLE, :], value_all[:, :, lo:hi], gate_all[:, :, lo:hi], ALU.mult)
+        for h1, (lo, hi) in zip(h1_parts, PICK_PARTS):
+            n = hi - lo
+            gate = pool.tile([P, PACK - WHOLE, n], F32, name="gate%d" % lo)
+            value = pool.tile([P, PACK - WHOLE, n], F32, name="value%d" % lo)
+            for t in range(WHOLE, PACK):
+                fetch(t, gate[:, t - WHOLE, :], value[:, t - WHOLE, :], slice(lo // 16, hi // 16))
+                nc.vector.tensor_tensor(h1[:, t, :], value[:, t - WHOLE, :], gate[:, t - WHOLE, :], ALU.mult)
+            h, o0 = divmod(lo // 2, half)
+            pairs = h1[:].rearrange("p t (o two) -> p two o t", two=2)
+            nc.vector.tensor_tensor(hid_bf[h][:, o0 : o0 + n // 2, :], pairs[:, 0], pairs[:, 1], ALU.max)
+            if o0 + n // 2 == half:
+                cols = slice(half * h, half * (h + 1))
+                nc.vector.quantize_mx(
+                    hid_words[:, cols].bitcast(E5M2), hid_plane[:, cols],
+                    hid_bf[h][:].rearrange("p o t -> p (o t)"),
+                )
+
+        for h in range(N // P):
+            cols = slice(P * h, P * (h + 1))
+            nc.tensor.matmul_mx(
+                p_banks[h][:], lhsT=wb_sb[:, cols].bitcast(E4M3), lhsT_scale=wb_plane[:, cols],
+                rhs=hid_words[:].bitcast(E5M2), rhs_scale=hid_plane[:], start=False, stop=True,
+            )
+        p_rows = [pool.tile([P, O], F32, name="p_rows%d" % h) for h in range(N // P)]
+        nc.vector.tensor_copy(p_rows[0][:], p_banks[0][:])
+        nc.vector.tensor_copy(pages[0][:].indirect(list6[:]), p_rows[0][:])
+        nc.sync.dma_start(out[0:P, :], pages[0][:])
+        nc.scalar.copy(p_rows[1][:], p_banks[1][:])
+        nc.scalar.activation(pages[1][:].indirect(list6[:]), p_rows[1][:], ACT.Copy)
+        nc.scalar.dma_start(out[P : 2 * P, :], pages[1][:])

@@ -19,7 +19,7 @@ ALU = mybir.AluOpType
 
 P = 128
 PACK = 4
-WHOLE = 2
+WHOLE = 3
 PICK_PARTS = ((0, 128), (128, 192), (192, 256))
 
 
@@ -34,7 +34,7 @@ def tile_list_gatedpool_bank_further_scattered_kernel(
         psum = ctx.enter_context(tc.psum_pool(name="psum", bufs=1))
 
         def sbuf(name, shape, dtype):
-            return pool.tile(shape, dtype, name=name, align_bytes=64)
+            return pool.tile(shape, dtype, name=name, tag=name, align_bytes=64)
 
         def load_list(name, src):
             tile = pool.tile(list(src.shape), U16, name=name)
@@ -51,41 +51,57 @@ def tile_list_gatedpool_bank_further_scattered_kernel(
 
         def zeroed_plane(name, cols):
             tile = sbuf(name, [P, cols], U8)
-            nc.vector.memset(tile[:].bitcast(I32), 0)
+            nc.gpsimd.memset(tile[:].bitcast(I32), 0)
             return tile
 
         def load_plane(queue, tile, scales):
             for q in range(4):
                 queue.dma_start(tile[32 * q : 32 * q + 4, :].bitcast(I32), scales[0, 4 * q : 4 * q + 4, :].bitcast(I32))
 
+        def load_staged(queue, stage, c0, scales):
+            cols = scales.shape[2]
+            queue.dma_start(
+                stage[:, :, c0 // 4 : (c0 + cols) // 4], scales[0].bitcast(I32).rearrange("(q r) n -> r q n", r=4)
+            )
+
+        def spread(plane, stage):
+            for q in range(4):
+                nc.vector.tensor_copy(plane[32 * q : 32 * q + 4, :].bitcast(I32), stage[:, q, :])
+
+        def load_halves(stage, c0, scales):
+            cols = scales.shape[2]
+            rows = scales[0].bitcast(I32).rearrange("(h q r) n -> q r h n", h=2, q=2)
+            for q in range(2):
+                nc.sync.dma_start(stage[32 * q : 32 * q + 4, :, c0 // 4 : (c0 + cols) // 4], rows[q])
+
         def load_rows(name, src):
             tile = pool.tile([P, PACK], F32, name=name)
-            nc.gpsimd.dma_start(tile[:], src.rearrange("(p t) one -> p (t one)", t=PACK))
+            nc.sync.dma_start(tile[:], src.rearrange("(p t) one -> p (t one)", t=PACK))
             return tile
 
         xt_plane = zeroed_plane("xt_plane", T)
         xo_plane = zeroed_plane("xo_plane", Z)
-        w_plane = zeroed_plane("w_plane", R)
-        w0_plane = zeroed_plane("w0_plane", R)
         ws_plane = zeroed_plane("ws_plane", N)
         wb_plane = zeroed_plane("wb_plane", N)
-
-        xt_sb = load_words(nc.scalar, "xt_sb", xt_words[0], T, U16)
-        xo_sb = load_words(nc.scalar, "xo_sb", flat_words(xo_words), Z, U32)
-        w_sb = load_words(nc.scalar, "w_sb", flat_words(w_words), R, U32)
-        w0_sb = load_words(nc.scalar, "w0_sb", flat_words(w0_words), R, U32)
+        xo_stage = pool.tile([4, 4, Z // 4], I32, name="xo_stage")
+        ww_stage = pool.tile([64, 2, 2 * R // 4], I32, name="ww_stage")
+        nc.vector.memset(ww_stage[:], 0)
 
         list1 = load_list("list1", offs)
+        xt_sb = load_words(nc.sync, "xt_sb", xt_words[0], T, U16)
         load_plane(nc.sync, xt_plane, xt_scales)
         list2 = load_list("list2", offs2)
-        load_plane(nc.sync, xo_plane, xo_scales)
-        load_plane(nc.sync, w_plane, w_scales)
-        load_plane(nc.sync, w0_plane, w0_scales)
+        load_staged(nc.sync, xo_stage, 0, xo_scales)
+        w_sb = load_words(nc.sync, "w_sb", flat_words(w_words), R, U32)
+        load_halves(ww_stage, 0, w_scales)
+        load_halves(ww_stage, R, w0_scales)
+        xo_sb = load_words(nc.sync, "xo_sb", flat_words(xo_words), Z, U32)
+        w0_sb = load_words(nc.sync, "w0_sb", flat_words(w0_words), R, U32)
+        list4 = load_list("list4", offs4)
         sg_sb = load_rows("sg_sb", sg)
         bg_sb = load_rows("bg_sb", bg)
-        sa_sb = load_rows("sa_sb", sa)
-        list4 = load_list("list4", offs4)
         list3 = load_list("list3", offs3)
+        sa_sb = load_rows("sa_sb", sa)
         list5 = load_list("list5", offs5)
         ws_sb = load_words(nc.sync, "ws_sb", flat_words(ws_words), N, U32)
         wb_sb = load_words(nc.sync, "wb_sb", flat_words(wb_words), N, U32)
@@ -93,51 +109,58 @@ def tile_list_gatedpool_bank_further_scattered_kernel(
         load_plane(nc.sync, wb_plane, wb_scales)
         list6 = load_list("list6", offs6)
 
-        pages = [pool.tile([P, E], F32, name="page%d" % h) for h in range(N // P)]
-        for page in pages:
-            nc.vector.memset(page[:], 0.0)
-
-        def gather(name, table, offsets, cols, dtype):
-            tile = sbuf(name, [P, cols], dtype)
+        def gather(name, table, offsets, cols, dtype, tag=""):
+            tile = pool.tile([P, cols], dtype, name=name, tag=tag or name, align_bytes=64)
             nc.vector.tensor_copy(tile[:], table[:].indirect(offsets[:]))
             return tile
 
-        def deal(copy, name, src, dtype, run, t0, t1):
-            tile = sbuf(name, [P, (t1 - t0) * P], dtype)
-            copy(
-                tile[:].rearrange("p (t c i) -> p c t i", t=t1 - t0, i=run),
-                src[:].rearrange("p (c i t) -> p c t i", t=PACK, i=run)[:, :, t0:t1, :],
-            )
-            return [tile[:, P * t : P * (t + 1)] for t in range(t1 - t0)]
+        def deal_words(name, src, t0, t1):
+            tile = sbuf(name, [P, t1 - t0, P], U32)
+            nc.scalar.copy(tile[:].rearrange("p t m -> p m t"), src[:].rearrange("p (m t) -> p m t", t=PACK)[:, :, t0:t1])
+            return [tile[:, t, :] for t in range(t1 - t0)]
 
-        xt1_plane = gather("xt1_plane", xt_plane, list1, J, U8)
+        def deal_scales(t):
+            dealt = pool.tile([P, 2 * P], U8, name="dealt", bufs=2, align_bytes=64)
+            nc.vector.tensor_copy(dealt[:], ww_plane[:, t::PACK])
+            return dealt
+
         xt1_words = gather("xt1_words", xt_sb, list1, J, U16)
+        xt1_plane = gather("xt1_plane", xt_plane, list1, J, U8)
+        spread(xo_plane, xo_stage)
         xo2_plane = gather("xo2_plane", xo_plane, list2, J, U8)
+        ww_plane = sbuf("ww_plane", [P, 2 * R], U8)
+        for h in range(2):
+            nc.vector.tensor_copy(ww_plane[64 * h : 64 * (h + 1), :].bitcast(I32), ww_stage[:, h, :])
+        dealt = deal_scales(0)
         xo2_words = gather("xo2_words", xo_sb, list2, J, U32)
-        wd_words = deal(nc.scalar.copy, "wd_words", w_sb, U32, 4, 0, PACK)
-        wd_plane, w0d_plane, w0d_words = [], [], []
-        for t0, t1 in ((0, 1), (1, PACK)):
-            wd_plane.extend(deal(nc.vector.tensor_copy, "wd_plane%d" % t0, w_plane, U8, 16, t0, t1))
-            w0d_plane.extend(deal(nc.vector.tensor_copy, "w0d_plane%d" % t0, w0_plane, U8, 16, t0, t1))
-            w0d_words.extend(deal(nc.scalar.copy, "w0d_words%d" % t0, w0_sb, U32, 4, t0, t1))
+        wd_words = deal_words("wd_words", w_sb, 0, PACK)
+        w0d_words = deal_words("w0d_first", w0_sb, 0, 1) + deal_words("w0d_rest", w0_sb, 1, PACK)
 
         a_rows = []
         for t in range(PACK):
+            if t > 0:
+                dealt = deal_scales(t)
             bank = psum.tile([P, J], F32, name="a_bank%d" % t)
             nc.tensor.matmul_mx(
-                bank[:], lhsT=wd_words[t].bitcast(E5M2), lhsT_scale=wd_plane[t],
+                bank[:], lhsT=wd_words[t].bitcast(E5M2), lhsT_scale=dealt[:, 0:P],
                 rhs=xt1_words[:].bitcast(E2M1), rhs_scale=xt1_plane[:], start=True, stop=False,
             )
             nc.tensor.matmul_mx(
-                bank[:], lhsT=w0d_words[t].bitcast(E4M3), lhsT_scale=w0d_plane[t],
+                bank[:], lhsT=w0d_words[t].bitcast(E4M3), lhsT_scale=dealt[:, P : 2 * P],
                 rhs=xo2_words[:].bitcast(E5M2), rhs_scale=xo2_plane[:], start=False, stop=True,
             )
             rows = pool.tile([P, 2 * J if t < WHOLE else J], F32, name="a_rows%d" % t)
             nc.vector.tensor_copy(rows[:, 0:J], bank[:])
             a_rows.append(rows)
 
-        xt5_plane = gather("xt5_plane", xt_plane, list5, O, U8)
-        xt5_words = gather("xt5_words", xt_sb, list5, O, U16)
+        pages = []
+        for tag in ("wd_words", "w0d_rest"):
+            page = pool.tile([P, E], F32, name="page_" + tag, tag=tag, align_bytes=64)
+            nc.gpsimd.memset(page[:], 0.0)
+            pages.append(page)
+
+        xt5_plane = gather("xt5_plane", xt_plane, list5, O, U8, tag="xt1_plane")
+        xt5_words = gather("xt5_words", xt_sb, list5, O, U16, tag="xt1_words")
         p_banks = [psum.tile([P, O], F32, name="p_bank%d" % h) for h in range(N // P)]
         for h in range(N // P):
             cols = slice(P * h, P * (h + 1))
@@ -165,8 +188,8 @@ def tile_list_gatedpool_bank_further_scattered_kernel(
         value_all = pool.tile([P, WHOLE, I], F32, name="value_all")
         for t in range(WHOLE):
             fetch(t, gate_all[:, t, :], value_all[:, t, :], slice(0, I // 16))
-        for h1, (lo, hi) in zip(h1_parts, PICK_PARTS):
-            nc.vector.tensor_tensor(h1[:, 0:WHOLE, :], value_all[:, :, lo:hi], gate_all[:, :, lo:hi], ALU.mult)
+            for h1, (lo, hi) in zip(h1_parts, PICK_PARTS):
+                nc.vector.tensor_tensor(h1[:, t, :], value_all[:, t, lo:hi], gate_all[:, t, lo:hi], ALU.mult)
         for h1, (lo, hi) in zip(h1_parts, PICK_PARTS):
             n = hi - lo
             gate = pool.tile([P, PACK - WHOLE, n], F32, name="gate%d" % lo)

@@ -49,24 +49,14 @@ def tile_list_gatedpool_bank_further_scattered_kernel(
         def flat_words(words):
             return words[0].rearrange("p n t -> p (n t)")
 
-        def zeroed_plane(name, cols):
+        def zeroed_plane(engine, name, cols):
             tile = sbuf(name, [P, cols], U8)
-            nc.gpsimd.memset(tile[:].bitcast(I32), 0)
+            engine.memset(tile[:].bitcast(I32), 0)
             return tile
 
-        def load_plane(queue, tile, scales):
-            for q in range(4):
+        def load_plane(tile, scales, queues):
+            for q, queue in enumerate(queues):
                 queue.dma_start(tile[32 * q : 32 * q + 4, :].bitcast(I32), scales[0, 4 * q : 4 * q + 4, :].bitcast(I32))
-
-        def load_staged(queue, stage, c0, scales):
-            cols = scales.shape[2]
-            queue.dma_start(
-                stage[:, :, c0 // 4 : (c0 + cols) // 4], scales[0].bitcast(I32).rearrange("(q r) n -> r q n", r=4)
-            )
-
-        def spread(plane, stage):
-            for q in range(4):
-                nc.vector.tensor_copy(plane[32 * q : 32 * q + 4, :].bitcast(I32), stage[:, q, :])
 
         def load_halves(stage, c0, scales):
             cols = scales.shape[2]
@@ -79,24 +69,23 @@ def tile_list_gatedpool_bank_further_scattered_kernel(
             nc.sync.dma_start(tile[:], src.rearrange("(p t) one -> p (t one)", t=PACK))
             return tile
 
-        xt_plane = zeroed_plane("xt_plane", T)
-        xo_plane = zeroed_plane("xo_plane", Z)
-        ws_plane = zeroed_plane("ws_plane", N)
-        wb_plane = zeroed_plane("wb_plane", N)
-        xo_stage = pool.tile([4, 4, Z // 4], I32, name="xo_stage")
+        xt_plane = zeroed_plane(nc.vector, "xt_plane", T)
+        xo_plane = zeroed_plane(nc.vector, "xo_plane", Z)
         ww_stage = pool.tile([64, 2, 2 * R // 4], I32, name="ww_stage")
         nc.vector.memset(ww_stage[:], 0)
 
+        w_sb = load_words(nc.gpsimd, "w_sb", flat_words(w_words), R, U32)
+        w0_sb = load_words(nc.gpsimd, "w0_sb", flat_words(w0_words), R, U32)
         list1 = load_list("list1", offs)
         xt_sb = load_words(nc.sync, "xt_sb", xt_words[0], T, U16)
-        load_plane(nc.sync, xt_plane, xt_scales)
+        load_plane(xt_plane, xt_scales, [nc.sync] * 4)
         list2 = load_list("list2", offs2)
-        load_staged(nc.sync, xo_stage, 0, xo_scales)
-        w_sb = load_words(nc.sync, "w_sb", flat_words(w_words), R, U32)
+        xo_sb = load_words(nc.sync, "xo_sb", flat_words(xo_words), Z, U32)
         load_halves(ww_stage, 0, w_scales)
         load_halves(ww_stage, R, w0_scales)
-        xo_sb = load_words(nc.sync, "xo_sb", flat_words(xo_words), Z, U32)
-        w0_sb = load_words(nc.sync, "w0_sb", flat_words(w0_words), R, U32)
+        load_plane(xo_plane, xo_scales, [nc.sync] * 3 + [nc.gpsimd])
+        ws_plane = zeroed_plane(nc.gpsimd, "ws_plane", N)
+        wb_plane = zeroed_plane(nc.gpsimd, "wb_plane", N)
         list4 = load_list("list4", offs4)
         sg_sb = load_rows("sg_sb", sg)
         bg_sb = load_rows("bg_sb", bg)
@@ -105,8 +94,8 @@ def tile_list_gatedpool_bank_further_scattered_kernel(
         list5 = load_list("list5", offs5)
         ws_sb = load_words(nc.sync, "ws_sb", flat_words(ws_words), N, U32)
         wb_sb = load_words(nc.sync, "wb_sb", flat_words(wb_words), N, U32)
-        load_plane(nc.sync, ws_plane, ws_scales)
-        load_plane(nc.sync, wb_plane, wb_scales)
+        load_plane(ws_plane, ws_scales, [nc.sync] * 4)
+        load_plane(wb_plane, wb_scales, [nc.sync] * 4)
         list6 = load_list("list6", offs6)
 
         def gather(name, table, offsets, cols, dtype, tag=""):
@@ -126,13 +115,12 @@ def tile_list_gatedpool_bank_further_scattered_kernel(
 
         xt1_words = gather("xt1_words", xt_sb, list1, J, U16)
         xt1_plane = gather("xt1_plane", xt_plane, list1, J, U8)
-        spread(xo_plane, xo_stage)
-        xo2_plane = gather("xo2_plane", xo_plane, list2, J, U8)
+        xo2_words = gather("xo2_words", xo_sb, list2, J, U32)
         ww_plane = sbuf("ww_plane", [P, 2 * R], U8)
         for h in range(2):
             nc.vector.tensor_copy(ww_plane[64 * h : 64 * (h + 1), :].bitcast(I32), ww_stage[:, h, :])
         dealt = deal_scales(0)
-        xo2_words = gather("xo2_words", xo_sb, list2, J, U32)
+        xo2_plane = gather("xo2_plane", xo_plane, list2, J, U8)
         wd_words = deal_words("wd_words", w_sb, 0, PACK)
         w0d_words = deal_words("w0d_first", w0_sb, 0, 1) + deal_words("w0d_rest", w0_sb, 1, PACK)
 
@@ -153,12 +141,6 @@ def tile_list_gatedpool_bank_further_scattered_kernel(
             nc.vector.tensor_copy(rows[:, 0:J], bank[:])
             a_rows.append(rows)
 
-        pages = []
-        for tag in ("wd_words", "w0d_rest"):
-            page = pool.tile([P, E], F32, name="page_" + tag, tag=tag, align_bytes=64)
-            nc.gpsimd.memset(page[:], 0.0)
-            pages.append(page)
-
         xt5_plane = gather("xt5_plane", xt_plane, list5, O, U8, tag="xt1_plane")
         xt5_words = gather("xt5_words", xt_sb, list5, O, U16, tag="xt1_words")
         p_banks = [psum.tile([P, O], F32, name="p_bank%d" % h) for h in range(N // P)]
@@ -169,41 +151,53 @@ def tile_list_gatedpool_bank_further_scattered_kernel(
                 rhs=xt5_words[:].bitcast(E2M1), rhs_scale=xt5_plane[:], start=True, stop=False,
             )
 
+        pages = []
+        for tag in ("xt_sb", "xt1_plane"):
+            page = pool.tile([P, E], F32, name="page_" + tag, tag=tag, align_bytes=64)
+            nc.gpsimd.memset(page[:], 0.0)
+            pages.append(page)
+
         hid_words = sbuf("hid_words", [P, O], U32)
         hid_plane = sbuf("hid_plane", [P, O], U8)
         half = O // 2
         hid_bf = [sbuf("hid_bf%d" % h, [P, half, PACK], BF16) for h in range(2)]
 
-        def fetch(t, gate, value, entries):
+        gate = pool.tile([P, PACK, I], F32, name="gate")
+        value = pool.tile([P, PACK, I], F32, name="value")
+        h1 = pool.tile([P, PACK, I], F32, name="h1")
+        pairs = h1[:].rearrange("p t (o two) -> p two o t", two=2)
+
+        def gated_picks(t, lo, hi):
+            entries = slice(lo // 16, hi // 16)
             nc.scalar.activation(
-                gate, a_rows[t][:].indirect(list4[:, entries]), ACT.Sigmoid,
+                gate[:, t, lo:hi], a_rows[t][:].indirect(list4[:, entries]), ACT.Sigmoid,
                 bias=bg_sb[:, t : t + 1], scale=sg_sb[:, t : t + 1],
             )
             nc.scalar.activation(
-                value, a_rows[t][:].indirect(list3[:, entries]), ACT.Copy, scale=sa_sb[:, t : t + 1],
+                value[:, t, lo:hi], a_rows[t][:].indirect(list3[:, entries]), ACT.Copy, scale=sa_sb[:, t : t + 1],
+            )
+            nc.vector.tensor_tensor(h1[:, t, lo:hi], value[:, t, lo:hi], gate[:, t, lo:hi], ALU.mult)
+
+        def pooled(o_lo, o_hi, t0):
+            h, o0 = divmod(o_lo, half)
+            nc.vector.tensor_tensor(
+                hid_bf[h][:, o0 : o0 + o_hi - o_lo, t0 : t0 + 2],
+                pairs[:, 0, o_lo:o_hi, t0 : t0 + 2], pairs[:, 1, o_lo:o_hi, t0 : t0 + 2], ALU.max,
             )
 
-        h1_parts = [pool.tile([P, PACK, hi - lo], F32, name="h1_%d" % lo) for lo, hi in PICK_PARTS]
-        gate_all = pool.tile([P, WHOLE, I], F32, name="gate_all")
-        value_all = pool.tile([P, WHOLE, I], F32, name="value_all")
-        for t in range(WHOLE):
-            fetch(t, gate_all[:, t, :], value_all[:, t, :], slice(0, I // 16))
-            for h1, (lo, hi) in zip(h1_parts, PICK_PARTS):
-                nc.vector.tensor_tensor(h1[:, t, :], value_all[:, t, lo:hi], gate_all[:, t, lo:hi], ALU.mult)
-        for h1, (lo, hi) in zip(h1_parts, PICK_PARTS):
-            n = hi - lo
-            gate = pool.tile([P, PACK - WHOLE, n], F32, name="gate%d" % lo)
-            value = pool.tile([P, PACK - WHOLE, n], F32, name="value%d" % lo)
-            for t in range(WHOLE, PACK):
-                fetch(t, gate[:, t - WHOLE, :], value[:, t - WHOLE, :], slice(lo // 16, hi // 16))
-                nc.vector.tensor_tensor(h1[:, t, :], value[:, t - WHOLE, :], gate[:, t - WHOLE, :], ALU.mult)
-            h, o0 = divmod(lo // 2, half)
-            pairs = h1[:].rearrange("p t (o two) -> p two o t", two=2)
-            nc.vector.tensor_tensor(hid_bf[h][:, o0 : o0 + n // 2, :], pairs[:, 0], pairs[:, 1], ALU.max)
-            if o0 + n // 2 == half:
-                cols = slice(half * h, half * (h + 1))
+        gated_picks(0, 0, I)
+        gated_picks(1, 0, I)
+        pooled(0, half, 0)
+        pooled(half, O, 0)
+        gated_picks(2, 0, I)
+        for lo, hi in PICK_PARTS:
+            gated_picks(3, lo, hi)
+            pooled(lo // 2, hi // 2, 2)
+            if hi // 2 % half == 0:
+                h = lo // 2 // half
+                pools = slice(half * h, half * (h + 1))
                 nc.vector.quantize_mx(
-                    hid_words[:, cols].bitcast(E5M2), hid_plane[:, cols],
+                    hid_words[:, pools].bitcast(E5M2), hid_plane[:, pools],
                     hid_bf[h][:].rearrange("p o t -> p (o t)"),
                 )
 

@@ -19,7 +19,8 @@ ALU = mybir.AluOpType
 
 P = 128
 PACK = 4
-WHOLE = 3
+QUADS = 4
+LAST = PACK - 1
 PICK_PARTS = ((0, 128), (128, 192), (192, 256))
 
 
@@ -33,8 +34,8 @@ def tile_list_gatedpool_bank_further_scattered_kernel(
         pool = ctx.enter_context(tc.tile_pool(name="held", bufs=1))
         psum = ctx.enter_context(tc.psum_pool(name="psum", bufs=1))
 
-        def sbuf(name, shape, dtype):
-            return pool.tile(shape, dtype, name=name, tag=name, align_bytes=64)
+        def aligned(name, shape, dtype, tag=""):
+            return pool.tile(shape, dtype, name=name, tag=tag or name, align_bytes=64)
 
         def load_list(name, src):
             tile = pool.tile(list(src.shape), U16, name=name)
@@ -42,71 +43,76 @@ def tile_list_gatedpool_bank_further_scattered_kernel(
             return tile
 
         def load_words(queue, name, src, cols, dtype):
-            tile = sbuf(name, [P, cols], dtype)
+            tile = aligned(name, [P, cols], dtype)
             queue.dma_start(tile[:].bitcast(I32), src.bitcast(I32))
             return tile
 
         def flat_words(words):
             return words[0].rearrange("p n t -> p (n t)")
 
-        def zeroed_plane(engine, name, cols):
-            tile = sbuf(name, [P, cols], U8)
-            engine.memset(tile[:].bitcast(I32), 0)
+        def zeroed_plane(name, cols):
+            tile = aligned(name, [P, cols], U8)
+            nc.gpsimd.memset(tile[:].bitcast(I32), 0)
             return tile
 
-        def load_plane(tile, scales, queues):
-            for q, queue in enumerate(queues):
-                queue.dma_start(tile[32 * q : 32 * q + 4, :].bitcast(I32), scales[0, 4 * q : 4 * q + 4, :].bitcast(I32))
+        def load_plane(plane, scales):
+            for q in range(QUADS):
+                nc.sync.dma_start(
+                    plane[32 * q : 32 * q + 4, :].bitcast(I32), scales[0, 4 * q : 4 * q + 4, :].bitcast(I32)
+                )
 
         def load_halves(stage, c0, scales):
             cols = scales.shape[2]
-            rows = scales[0].bitcast(I32).rearrange("(h q r) n -> q r h n", h=2, q=2)
+            rows = scales[0].bitcast(I32).rearrange("(h q s) n -> q s h n", h=2, q=2)
             for q in range(2):
                 nc.sync.dma_start(stage[32 * q : 32 * q + 4, :, c0 // 4 : (c0 + cols) // 4], rows[q])
 
-        def load_rows(name, src):
+        def load_row_factors(name, src):
             tile = pool.tile([P, PACK], F32, name=name)
-            nc.sync.dma_start(tile[:], src.rearrange("(p t) one -> p (t one)", t=PACK))
+            nc.gpsimd.dma_start(tile[:], src.rearrange("(p t) one -> p (t one)", t=PACK))
             return tile
 
-        xt_plane = zeroed_plane(nc.vector, "xt_plane", T)
-        xo_plane = zeroed_plane(nc.vector, "xo_plane", Z)
+        xt_plane = zeroed_plane("xt_plane", T)
+        w0_sb = load_words(nc.gpsimd, "w0_sb", flat_words(w0_words), R, U32)
+        xo_plane = zeroed_plane("xo_plane", Z)
+        ws_plane = zeroed_plane("ws_plane", N)
+        wb_plane = zeroed_plane("wb_plane", N)
+        xo_stage = pool.tile([4, QUADS, Z // 4], I32, name="xo_stage")
         ww_stage = pool.tile([64, 2, 2 * R // 4], I32, name="ww_stage")
         nc.vector.memset(ww_stage[:], 0)
 
-        w_sb = load_words(nc.gpsimd, "w_sb", flat_words(w_words), R, U32)
-        w0_sb = load_words(nc.gpsimd, "w0_sb", flat_words(w0_words), R, U32)
         list1 = load_list("list1", offs)
         xt_sb = load_words(nc.sync, "xt_sb", xt_words[0], T, U16)
-        load_plane(xt_plane, xt_scales, [nc.sync] * 4)
+        load_plane(xt_plane, xt_scales)
         list2 = load_list("list2", offs2)
-        xo_sb = load_words(nc.sync, "xo_sb", flat_words(xo_words), Z, U32)
+        nc.sync.dma_start(xo_stage[:], xo_scales[0].bitcast(I32).rearrange("(q s) n -> s q n", s=4))
+        w_sb = load_words(nc.sync, "w_sb", flat_words(w_words), R, U32)
         load_halves(ww_stage, 0, w_scales)
         load_halves(ww_stage, R, w0_scales)
-        load_plane(xo_plane, xo_scales, [nc.sync] * 3 + [nc.gpsimd])
-        ws_plane = zeroed_plane(nc.gpsimd, "ws_plane", N)
-        wb_plane = zeroed_plane(nc.gpsimd, "wb_plane", N)
+        xo_sb = load_words(nc.sync, "xo_sb", flat_words(xo_words), Z, U32)
         list4 = load_list("list4", offs4)
-        sg_sb = load_rows("sg_sb", sg)
-        bg_sb = load_rows("bg_sb", bg)
+        sg_sb = load_row_factors("sg_sb", sg)
+        bg_sb = load_row_factors("bg_sb", bg)
         list3 = load_list("list3", offs3)
-        sa_sb = load_rows("sa_sb", sa)
+        sa_sb = load_row_factors("sa_sb", sa)
         list5 = load_list("list5", offs5)
         ws_sb = load_words(nc.sync, "ws_sb", flat_words(ws_words), N, U32)
         wb_sb = load_words(nc.sync, "wb_sb", flat_words(wb_words), N, U32)
-        load_plane(ws_plane, ws_scales, [nc.sync] * 4)
-        load_plane(wb_plane, wb_scales, [nc.sync] * 4)
+        load_plane(ws_plane, ws_scales)
+        load_plane(wb_plane, wb_scales)
         list6 = load_list("list6", offs6)
 
         def gather(name, table, offsets, cols, dtype, tag=""):
-            tile = pool.tile([P, cols], dtype, name=name, tag=tag or name, align_bytes=64)
+            tile = aligned(name, [P, cols], dtype, tag)
             nc.vector.tensor_copy(tile[:], table[:].indirect(offsets[:]))
             return tile
 
         def deal_words(name, src, t0, t1):
-            tile = sbuf(name, [P, t1 - t0, P], U32)
-            nc.scalar.copy(tile[:].rearrange("p t m -> p m t"), src[:].rearrange("p (m t) -> p m t", t=PACK)[:, :, t0:t1])
-            return [tile[:, t, :] for t in range(t1 - t0)]
+            tile = aligned(name, [P, t1 - t0, P], U32)
+            nc.scalar.copy(
+                tile[:].rearrange("p t m -> p m t"), src[:].rearrange("p (m t) -> p m t", t=PACK)[:, :, t0:t1]
+            )
+            return [tile[:, u, :] for u in range(t1 - t0)]
 
         def deal_scales(t):
             dealt = pool.tile([P, 2 * P], U8, name="dealt", bufs=2, align_bytes=64)
@@ -115,12 +121,14 @@ def tile_list_gatedpool_bank_further_scattered_kernel(
 
         xt1_words = gather("xt1_words", xt_sb, list1, J, U16)
         xt1_plane = gather("xt1_plane", xt_plane, list1, J, U8)
-        xo2_words = gather("xo2_words", xo_sb, list2, J, U32)
-        ww_plane = sbuf("ww_plane", [P, 2 * R], U8)
+        for q in range(QUADS):
+            nc.vector.tensor_copy(xo_plane[32 * q : 32 * q + 4, :].bitcast(I32), xo_stage[:, q, :])
+        xo2_plane = gather("xo2_plane", xo_plane, list2, J, U8)
+        ww_plane = aligned("ww_plane", [P, 2 * R], U8)
         for h in range(2):
             nc.vector.tensor_copy(ww_plane[64 * h : 64 * (h + 1), :].bitcast(I32), ww_stage[:, h, :])
         dealt = deal_scales(0)
-        xo2_plane = gather("xo2_plane", xo_plane, list2, J, U8)
+        xo2_words = gather("xo2_words", xo_sb, list2, J, U32)
         wd_words = deal_words("wd_words", w_sb, 0, PACK)
         w0d_words = deal_words("w0d_first", w0_sb, 0, 1) + deal_words("w0d_rest", w0_sb, 1, PACK)
 
@@ -137,12 +145,12 @@ def tile_list_gatedpool_bank_further_scattered_kernel(
                 bank[:], lhsT=w0d_words[t].bitcast(E4M3), lhsT_scale=dealt[:, P : 2 * P],
                 rhs=xo2_words[:].bitcast(E5M2), rhs_scale=xo2_plane[:], start=False, stop=True,
             )
-            rows = pool.tile([P, 2 * J if t < WHOLE else J], F32, name="a_rows%d" % t)
+            rows = pool.tile([P, J if t == LAST else 2 * J], F32, name="a_rows%d" % t)
             nc.vector.tensor_copy(rows[:, 0:J], bank[:])
             a_rows.append(rows)
 
-        xt5_plane = gather("xt5_plane", xt_plane, list5, O, U8, tag="xt1_plane")
-        xt5_words = gather("xt5_words", xt_sb, list5, O, U16, tag="xt1_words")
+        xt5_plane = gather("xt5_plane", xt_plane, list5, O, U8, tag="xo2_plane")
+        xt5_words = gather("xt5_words", xt_sb, list5, O, U16, tag="xo2_words")
         p_banks = [psum.tile([P, O], F32, name="p_bank%d" % h) for h in range(N // P)]
         for h in range(N // P):
             cols = slice(P * h, P * (h + 1))
@@ -152,19 +160,19 @@ def tile_list_gatedpool_bank_further_scattered_kernel(
             )
 
         pages = []
-        for tag in ("xt_sb", "xt1_plane"):
-            page = pool.tile([P, E], F32, name="page_" + tag, tag=tag, align_bytes=64)
+        for tag in ("xt_sb", "xo2_plane"):
+            page = aligned("page_" + tag, [P, E], F32, tag)
             nc.gpsimd.memset(page[:], 0.0)
             pages.append(page)
 
-        hid_words = sbuf("hid_words", [P, O], U32)
-        hid_plane = sbuf("hid_plane", [P, O], U8)
+        hid_words = aligned("hid_words", [P, O], U32)
+        hid_plane = aligned("hid_plane", [P, O], U8)
         half = O // 2
-        hid_bf = [sbuf("hid_bf%d" % h, [P, half, PACK], BF16) for h in range(2)]
+        hid_bf = [aligned("hid_bf%d" % h, [P, half, PACK], BF16) for h in range(2)]
 
         gate = pool.tile([P, PACK, I], F32, name="gate")
         value = pool.tile([P, PACK, I], F32, name="value")
-        h1 = pool.tile([P, PACK, I], F32, name="h1")
+        h1 = aligned("h1", [P, PACK, I], F32, tag="w0d_rest")
         pairs = h1[:].rearrange("p t (o two) -> p two o t", two=2)
 
         def gated_picks(t, lo, hi):
@@ -191,7 +199,7 @@ def tile_list_gatedpool_bank_further_scattered_kernel(
         pooled(half, O, 0)
         gated_picks(2, 0, I)
         for lo, hi in PICK_PARTS:
-            gated_picks(3, lo, hi)
+            gated_picks(LAST, lo, hi)
             pooled(lo // 2, hi // 2, 2)
             if hi // 2 % half == 0:
                 h = lo // 2 // half

from contextlib import ExitStack

import concourse.mybir as mybir

K, T, J, R, F, Z, I, O, N, E = 512, 1024, 256, 512, 512, 1024, 256, 128, 256, 1024
FLOPS = 2 * (K * R * J + F * R * J + R * N * O + K * N * O)

F32 = mybir.dt.float32
BF16 = mybir.dt.bfloat16
I32 = mybir.dt.int32
U32 = mybir.dt.uint32
U16 = mybir.dt.uint16
U8 = mybir.dt.uint8
E4M3 = mybir.dt.float8_e4m3fn_x4
E5M2 = mybir.dt.float8_e5m2_x4
E2M1 = mybir.dt.float4_e2m1fn_x4
ACT = mybir.ActivationFunctionType
ALU = mybir.AluOpType

P = 128
PACK = 4
QUADS = 4
LAST = PACK - 1
PICK_PARTS = ((0, 128), (128, 192), (192, 256))


def tile_list_gatedpool_bank_further_scattered_kernel(
    tc, xt_words, xt_scales, xo_words, xo_scales, w_words, w_scales, w0_words, w0_scales,
    sa, sg, bg, wb_words, wb_scales, ws_words, ws_scales,
    offs, offs2, offs3, offs4, offs5, offs6, out,
):
    nc = tc.nc
    with ExitStack() as ctx:
        pool = ctx.enter_context(tc.tile_pool(name="held", bufs=1))
        psum = ctx.enter_context(tc.psum_pool(name="psum", bufs=1))

        def aligned(name, shape, dtype, tag=""):
            return pool.tile(shape, dtype, name=name, tag=tag or name, align_bytes=64)

        def load_list(name, src):
            tile = pool.tile(list(src.shape), U16, name=name)
            nc.sync.dma_start(tile[:], src)
            return tile

        def load_words(queue, name, src, cols, dtype):
            tile = aligned(name, [P, cols], dtype)
            queue.dma_start(tile[:].bitcast(I32), src.bitcast(I32))
            return tile

        def flat_words(words):
            return words[0].rearrange("p n t -> p (n t)")

        def zeroed_plane(name, cols):
            tile = aligned(name, [P, cols], U8)
            nc.gpsimd.memset(tile[:].bitcast(I32), 0)
            return tile

        def load_plane(plane, scales):
            for q in range(QUADS):
                nc.sync.dma_start(
                    plane[32 * q : 32 * q + 4, :].bitcast(I32), scales[0, 4 * q : 4 * q + 4, :].bitcast(I32)
                )

        def load_halves(stage, c0, scales):
            cols = scales.shape[2]
            rows = scales[0].bitcast(I32).rearrange("(h q s) n -> q s h n", h=2, q=2)
            for q in range(2):
                nc.sync.dma_start(stage[32 * q : 32 * q + 4, :, c0 // 4 : (c0 + cols) // 4], rows[q])

        def load_row_factors(name, src):
            tile = pool.tile([P, PACK], F32, name=name)
            nc.gpsimd.dma_start(tile[:], src.rearrange("(p t) one -> p (t one)", t=PACK))
            return tile

        xt_plane = zeroed_plane("xt_plane", T)
        w0_sb = load_words(nc.gpsimd, "w0_sb", flat_words(w0_words), R, U32)
        xo_plane = zeroed_plane("xo_plane", Z)
        ws_plane = zeroed_plane("ws_plane", N)
        wb_plane = zeroed_plane("wb_plane", N)
        xo_stage = pool.tile([4, QUADS, Z // 4], I32, name="xo_stage")
        ww_stage = pool.tile([64, 2, 2 * R // 4], I32, name="ww_stage")
        nc.vector.memset(ww_stage[:], 0)

        list1 = load_list("list1", offs)
        xt_sb = load_words(nc.sync, "xt_sb", xt_words[0], T, U16)
        load_plane(xt_plane, xt_scales)
        list2 = load_list("list2", offs2)
        nc.sync.dma_start(xo_stage[:], xo_scales[0].bitcast(I32).rearrange("(q s) n -> s q n", s=4))
        w_sb = load_words(nc.sync, "w_sb", flat_words(w_words), R, U32)
        load_halves(ww_stage, 0, w_scales)
        load_halves(ww_stage, R, w0_scales)
        xo_sb = load_words(nc.sync, "xo_sb", flat_words(xo_words), Z, U32)
        list4 = load_list("list4", offs4)
        sg_sb = load_row_factors("sg_sb", sg)
        bg_sb = load_row_factors("bg_sb", bg)
        list3 = load_list("list3", offs3)
        sa_sb = load_row_factors("sa_sb", sa)
        list5 = load_list("list5", offs5)
        ws_sb = load_words(nc.sync, "ws_sb", flat_words(ws_words), N, U32)
        wb_sb = load_words(nc.sync, "wb_sb", flat_words(wb_words), N, U32)
        load_plane(ws_plane, ws_scales)
        load_plane(wb_plane, wb_scales)
        list6 = load_list("list6", offs6)

        def gather(name, table, offsets, cols, dtype, tag=""):
            tile = aligned(name, [P, cols], dtype, tag)
            nc.vector.tensor_copy(tile[:], table[:].indirect(offsets[:]))
            return tile

        def deal_words(name, src, t0, t1):
            tile = aligned(name, [P, t1 - t0, P], U32)
            nc.scalar.copy(
                tile[:].rearrange("p t m -> p m t"), src[:].rearrange("p (m t) -> p m t", t=PACK)[:, :, t0:t1]
            )
            return [tile[:, u, :] for u in range(t1 - t0)]

        def deal_scales(t):
            dealt = pool.tile([P, 2 * P], U8, name="dealt", bufs=2, align_bytes=64)
            nc.vector.tensor_copy(dealt[:], ww_plane[:, t::PACK])
            return dealt

        xt1_words = gather("xt1_words", xt_sb, list1, J, U16)
        xt1_plane = gather("xt1_plane", xt_plane, list1, J, U8)
        for q in range(QUADS):
            nc.vector.tensor_copy(xo_plane[32 * q : 32 * q + 4, :].bitcast(I32), xo_stage[:, q, :])
        xo2_plane = gather("xo2_plane", xo_plane, list2, J, U8)
        ww_plane = aligned("ww_plane", [P, 2 * R], U8)
        for h in range(2):
            nc.vector.tensor_copy(ww_plane[64 * h : 64 * (h + 1), :].bitcast(I32), ww_stage[:, h, :])
        dealt = deal_scales(0)
        xo2_words = gather("xo2_words", xo_sb, list2, J, U32)
        wd_words = deal_words("wd_words", w_sb, 0, PACK)
        w0d_words = deal_words("w0d_first", w0_sb, 0, 1) + deal_words("w0d_rest", w0_sb, 1, PACK)

        a_rows = []
        for t in range(PACK):
            if t > 0:
                dealt = deal_scales(t)
            bank = psum.tile([P, J], F32, name="a_bank%d" % t)
            nc.tensor.matmul_mx(
                bank[:], lhsT=wd_words[t].bitcast(E5M2), lhsT_scale=dealt[:, 0:P],
                rhs=xt1_words[:].bitcast(E2M1), rhs_scale=xt1_plane[:], start=True, stop=False,
            )
            nc.tensor.matmul_mx(
                bank[:], lhsT=w0d_words[t].bitcast(E4M3), lhsT_scale=dealt[:, P : 2 * P],
                rhs=xo2_words[:].bitcast(E5M2), rhs_scale=xo2_plane[:], start=False, stop=True,
            )
            rows = pool.tile([P, J if t == LAST else 2 * J], F32, name="a_rows%d" % t)
            nc.vector.tensor_copy(rows[:, 0:J], bank[:])
            a_rows.append(rows)

        xt5_plane = gather("xt5_plane", xt_plane, list5, O, U8, tag="xo2_plane")
        xt5_words = gather("xt5_words", xt_sb, list5, O, U16, tag="xo2_words")
        p_banks = [psum.tile([P, O], F32, name="p_bank%d" % h) for h in range(N // P)]
        for h in range(N // P):
            cols = slice(P * h, P * (h + 1))
            nc.tensor.matmul_mx(
                p_banks[h][:], lhsT=ws_sb[:, cols].bitcast(E4M3), lhsT_scale=ws_plane[:, cols],
                rhs=xt5_words[:].bitcast(E2M1), rhs_scale=xt5_plane[:], start=True, stop=False,
            )

        pages = []
        for tag in ("xt_sb", "xo2_plane"):
            page = aligned("page_" + tag, [P, E], F32, tag)
            nc.gpsimd.memset(page[:], 0.0)
            pages.append(page)

        hid_words = aligned("hid_words", [P, O], U32)
        hid_plane = aligned("hid_plane", [P, O], U8)
        half = O // 2
        hid_bf = [aligned("hid_bf%d" % h, [P, half, PACK], BF16) for h in range(2)]

        gate = pool.tile([P, PACK, I], F32, name="gate")
        value = pool.tile([P, PACK, I], F32, name="value")
        h1 = aligned("h1", [P, PACK, I], F32, tag="w0d_rest")
        pairs = h1[:].rearrange("p t (o two) -> p two o t", two=2)

        def gated_picks(t, lo, hi):
            entries = slice(lo // 16, hi // 16)
            nc.scalar.activation(
                gate[:, t, lo:hi], a_rows[t][:].indirect(list4[:, entries]), ACT.Sigmoid,
                bias=bg_sb[:, t : t + 1], scale=sg_sb[:, t : t + 1],
            )
            nc.scalar.activation(
                value[:, t, lo:hi], a_rows[t][:].indirect(list3[:, entries]), ACT.Copy, scale=sa_sb[:, t : t + 1],
            )
            nc.vector.tensor_tensor(h1[:, t, lo:hi], value[:, t, lo:hi], gate[:, t, lo:hi], ALU.mult)

        def pooled(o_lo, o_hi, t0):
            h, o0 = divmod(o_lo, half)
            nc.vector.tensor_tensor(
                hid_bf[h][:, o0 : o0 + o_hi - o_lo, t0 : t0 + 2],
                pairs[:, 0, o_lo:o_hi, t0 : t0 + 2], pairs[:, 1, o_lo:o_hi, t0 : t0 + 2], ALU.max,
            )

        gated_picks(0, 0, I)
        gated_picks(1, 0, I)
        pooled(0, half, 0)
        pooled(half, O, 0)
        gated_picks(2, 0, I)
        for lo, hi in PICK_PARTS:
            gated_picks(LAST, lo, hi)
            pooled(lo // 2, hi // 2, 2)
            if hi // 2 % half == 0:
                h = lo // 2 // half
                pools = slice(half * h, half * (h + 1))
                nc.vector.quantize_mx(
                    hid_words[:, pools].bitcast(E5M2), hid_plane[:, pools],
                    hid_bf[h][:].rearrange("p o t -> p (o t)"),
                )

        for h in range(N // P):
            cols = slice(P * h, P * (h + 1))
            nc.tensor.matmul_mx(
                p_banks[h][:], lhsT=wb_sb[:, cols].bitcast(E4M3), lhsT_scale=wb_plane[:, cols],
                rhs=hid_words[:].bitcast(E5M2), rhs_scale=hid_plane[:], start=False, stop=True,
            )
        p_rows = [pool.tile([P, O], F32, name="p_rows%d" % h) for h in range(N // P)]
        nc.vector.tensor_copy(p_rows[0][:], p_banks[0][:])
        nc.vector.tensor_copy(pages[0][:].indirect(list6[:]), p_rows[0][:])
        nc.sync.dma_start(out[0:P, :], pages[0][:])
        nc.scalar.copy(p_rows[1][:], p_banks[1][:])
        nc.scalar.activation(pages[1][:].indirect(list6[:]), p_rows[1][:], ACT.Copy)
        nc.scalar.dma_start(out[P : 2 * P, :], pages[1][:])
